import numpy as np
import ml_dtypes

BF16 = ml_dtypes.bfloat16


def bf(x):
    return np.asarray(x, np.float32).astype(BF16)


def f32(x):
    return np.asarray(x, np.float32)


def f64(x):
    return np.asarray(x).astype(np.float64)


def striped(idx):
    return np.tile(idx.reshape(-1, 16).T, (8, 1))


S, K, M, N = 2048, 128, 256, 2048


def setup_inputs():
    return {"table": bf(np.random.standard_normal((S, K))), "w": bf(np.random.standard_normal((K, M)) / np.sqrt(K)), "offs": striped(np.random.permutation(S))}


def reference(table, w, offs):
    idx = offs[:16].T.reshape(-1)
    x = f64(table)[idx].T
    y = f64(w).T @ x
    return y

import concourse.mybir as mybir
from concourse.masks import make_identity

BF16, F32, U16 = mybir.dt.bfloat16, mybir.dt.float32, mybir.dt.uint16

P = 128
PIECE = 512
GROUP = 4

FLOPS = 2 * 2048 * 128 * 256


def tile_gather_matmul_kernel(tc, table, w, offs, out):
    nc = tc.nc
    tokens, features = table.shape
    outputs = w.shape[1]
    blocks = tokens // P

    def copy_out(turn, dst, src):
        if turn % 2 == 0:
            nc.vector.tensor_copy(dst, src)
        else:
            nc.scalar.copy(dst, src)

    with tc.tile_pool(name="held", bufs=1) as held, tc.tile_pool(name="staging", bufs=8) as staging:
        table_rows = held.tile([P, blocks, features], BF16)
        nc.sync.dma_start(table_rows[:], table.rearrange("(b p) k -> p b k", p=P))
        offsets = held.tile([P, tokens // 16], U16)
        nc.sync.dma_start(offsets[:], offs)
        weights = held.tile([P, outputs], BF16)
        nc.scalar.dma_start(weights[:], w)
        identity = held.tile([P, P], BF16)
        make_identity(nc, identity[:])

        table_cols = held.tile([P, tokens], BF16)
        with tc.psum_pool(name="flip", bufs=4) as flip:
            for g in range(blocks // GROUP):
                flipped = flip.tile([P, GROUP * P], BF16)
                for i in range(GROUP):
                    nc.tensor.transpose(
                        flipped[:, i * P : (i + 1) * P], table_rows[:, g * GROUP + i, :], identity[:]
                    )
                copy_out(g, table_cols[:, g * GROUP * P : (g + 1) * GROUP * P], flipped[:])

        with tc.psum_pool(name="sums", bufs=8) as sums:
            turn = 0
            for j in range(0, tokens, PIECE):
                picked = table_cols[:].indirect(offsets[:, j // 16 : (j + PIECE) // 16])
                for m in range(0, outputs, P):
                    y = sums.tile([P, PIECE], F32)
                    nc.tensor.matmul(y[:], weights[:, m : m + P], picked, start=True, stop=True)
                    y_sbuf = staging.tile([P, PIECE], F32)
                    copy_out(turn, y_sbuf[:], y[:])
                    nc.sync.dma_start(out[m : m + P, j : j + PIECE], y_sbuf[:])
                    turn += 1
